import numpy as np
import ml_dtypes


def mxq(x, axis, fmt="e4m3"):
    dtype, down = {"e4m3": (ml_dtypes.float8_e4m3fn, 7), "e5m2": (ml_dtypes.float8_e5m2, 14)}[fmt]
    v = np.moveaxis(np.asarray(x, np.float32).astype(ml_dtypes.bfloat16).astype(np.float64), axis, -1)
    blocks = v.reshape(v.shape[:-1] + (-1, 32))
    amax = np.abs(blocks).max(-1, keepdims=True)
    byte = np.maximum(np.where(amax > 0, np.frexp(amax)[1] - 1 + 127, 0) - down, 1)
    scale = np.exp2(byte - 127.0)
    codes = (blocks / scale).astype(np.float32).astype(dtype).astype(np.float64)
    return np.moveaxis((codes * scale).reshape(v.shape), -1, axis)


WIDE = False


def mx_kscale(k):
    if not WIDE:
        return np.ones(k)
    levels = np.array([10, -10, 5, -5, 0])
    if k % 512:
        return np.exp2(np.random.permutation(np.resize(levels, k // 32))).repeat(32)
    a = np.empty((k // 512, 16))
    for p in range(k // 512):
        a[p, :8] = np.random.permutation(np.resize(levels, 8))
        for g in range(8):
            far = levels[np.abs(levels - a[p, g]) >= 10]
            a[p, g + 8] = far[np.random.randint(len(far))]
    return np.exp2(a.ravel()).repeat(32)


def f64(x):
    return np.asarray(x).astype(np.float64)


def striped(idx):
    return np.tile(idx.reshape(-1, 16).T, (8, 1)).astype(np.uint16)


def unstriped(offs):
    return offs[:16].T.reshape(-1).astype(np.int64)


E2M1 = np.array([0.0, 0.5, 1.0, 1.5, 2.0, 3.0, 4.0, 6.0, -0.0, -0.5, -1.0, -1.5, -2.0, -3.0, -4.0, -6.0])


def pack_weight(w, fmt):
    k, n = w.shape
    w = f64(np.asarray(w, np.float32).astype(ml_dtypes.bfloat16)).reshape(k // 32, 32, n)
    amax = np.abs(w).max(1)
    if fmt == "e4m3":
        byte = np.frexp(amax)[1] - 1 + 127 - 7
    else:
        mant, ex = np.frexp(amax / 6.0)
        byte = np.where(mant > 0.5, ex, ex - 1) + 127
    byte = np.clip(np.where(amax > 0, byte, 1), 1, 254)
    scaled = (w * np.exp2(127.0 - byte)[:, None, :]).reshape(k, n).astype(np.float32)
    by_word = np.ascontiguousarray(scaled.reshape(k // 512, 128, 4, n).transpose(0, 1, 3, 2))
    if fmt == "e4m3":
        words = by_word.astype(ml_dtypes.float8_e4m3fn).view(np.uint8)
    else:
        c = by_word.astype(ml_dtypes.float4_e2m1fn).view(np.uint8) & 0xF
        words = (c[..., 0::2] | (c[..., 1::2] << 4)).reshape(k // 512, 128, 2 * n)
    return np.ascontiguousarray(words), np.ascontiguousarray(byte.astype(np.uint8).reshape(k // 512, 16, n))


def unpack_weight(words, scales, fmt):
    g, _, n = scales.shape
    words = np.ascontiguousarray(words).reshape(g, 128, n, -1)
    if fmt == "e4m3":
        vals = words.view(ml_dtypes.float8_e4m3fn).astype(np.float64)
    else:
        nib = np.empty((g, 128, n, 4), np.uint8)
        nib[..., 0::2] = words & 0xF
        nib[..., 1::2] = words >> 4
        vals = E2M1[nib]
    vals = vals * np.repeat(np.exp2(scales.astype(np.float64) - 127.0), 8, axis=1)[..., None]
    return vals.transpose(0, 1, 3, 2).reshape(g * 512, n)


def gelu(v):
    return 0.5 * v * (1.0 + np.tanh(np.sqrt(2.0 / np.pi) * (v + 0.044715 * v**3)))


def striped8(idx):
    return np.concatenate([v.reshape(-1, 16).T for v in idx]).astype(np.uint16)


def unstriped8(offs):
    return np.stack([offs[16 * g:16 * g + 16].T.reshape(-1) for g in range(8)]).astype(np.int64)


def heads(h, wgt, idx8):
    r = np.arange(h.shape[0])
    return wgt[r // 4 % 128] * h[r[:, None], idx8[r % 512 // 64]]


def put_heads(h, wgs, idx8, t2):
    r = np.arange(h.shape[0])
    page = np.zeros((h.shape[0], t2))
    page[r[:, None], idx8[r % 512 // 64]] = wgs[r // 4 % 128] * h
    return page


K, H, N, T, S, P, T2 = 1024, 1024, 512, 4096, 1024, 1024, 2048


def setup_inputs():
    n = np.random.standard_normal
    s = mx_kscale(K)[:, None]
    u = mx_kscale(H)[:, None]
    d = {}
    d["tab_words"], d["tab_scales"] = pack_weight(n((K, T)) * s, "e4m3")
    d["offs"] = striped(np.random.permutation(T)[:S])
    d["offs2"] = striped8(np.stack([np.random.permutation(T2)[:S] for _ in range(8)]))
    d["offs3"] = striped8(np.stack([np.random.permutation(T2)[:P] for _ in range(8)]))
    d["w1"] = (1.5 * n((K, H)) / K**0.5 / s).astype(np.float32)
    d["gain"] = (np.exp(0.3 * n(H)) * u[:, 0]).astype(np.float32)
    d["wgs"] = np.repeat(np.random.uniform(0.5, 2.0, (8, S)), 16, axis=0).astype(np.float32)
    d["wgt"] = np.repeat(np.random.uniform(0.5, 2.0, (8, P)), 16, axis=0).astype(np.float32)
    d["sense"] = (1.5 * np.exp(0.5 * n(H)) / u[:, 0]).astype(np.float32)
    d["cap"] = (n((H, P)) * u).astype(np.float32)
    d["w2_words"], d["w2_scales"] = pack_weight(1.8 * n((H, N)) / H**0.5 / u, "e2m1")
    d["w3"] = (1.3 * n((H, N)) / H**0.5 / u).astype(np.float32)
    return d


def reference(tab_words, tab_scales, offs, offs2, offs3, w1, gain, wgs, wgt, sense, cap, w2_words, w2_scales, w3):
    v = unpack_weight(tab_words, tab_scales, "e4m3")[:, unstriped(offs)]
    h = f64(gain)[:, None] * np.tanh(mxq(f64(w1), 0, "e4m3").T @ v)
    page = put_heads(h, f64(wgs), unstriped8(offs2), T2)
    x = heads(page, f64(wgt), unstriped8(offs3))
    z = f64(cap) / (1.0 + np.abs(f64(sense)[:, None] * x))
    w2 = unpack_weight(w2_words, w2_scales, "e2m1")
    room = w2.T @ mxq(z, 0, "e4m3")
    need = mxq(f64(w3), 0, "e4m3").T @ mxq(h, 0, "e4m3")
    return np.maximum(room, need)

@@ -1,0 +1,259 @@
+from contextlib import ExitStack
+
+import concourse.mybir as mybir
+
+K, H, N, T, S, T2 = 1024, 1024, 512, 4096, 1024, 2048
+FLOPS = 2 * K * H * S + 2 * 2 * H * N * S
+
+F32 = mybir.dt.float32
+BF16 = mybir.dt.bfloat16
+I32 = mybir.dt.int32
+U32 = mybir.dt.uint32
+U16 = mybir.dt.uint16
+U8 = mybir.dt.uint8
+FP8X4 = mybir.dt.float8_e4m3fn_x4
+FP4X4 = mybir.dt.float4_e2m1fn_x4
+ACT = mybir.ActivationFunctionType
+ALU = mybir.AluOpType
+
+P = 128
+PACK = 4
+PASS = P * PACK
+HALF = 512
+HALVES = S // HALF
+LIST_COLS = HALF // 16
+N_TILES = N // P
+
+
+def tile_list_locker_demand_scores_kernel(
+    tc, tab_words, tab_scales, offs, offs2, offs3, w1, gain, wgs, wgt, sense, cap, w2_words, w2_scales, w3, out
+):
+    nc = tc.nc
+    with ExitStack() as ctx:
+        keep = ctx.enter_context(tc.tile_pool(name="keep", bufs=1))
+        ring = ctx.enter_context(tc.tile_pool(name="ring", bufs=2))
+        psum = ctx.enter_context(tc.psum_pool(name="psum", bufs=8))
+
+        def held(shape, dtype, name, tag=None):
+            return keep.tile(shape, dtype, name=name, tag=tag or name, align_bytes=64)
+
+        def cols(half):
+            return slice(half * HALF, (half + 1) * HALF)
+
+        def entries(offsets, half):
+            return offsets[:, half * LIST_COLS : (half + 1) * LIST_COLS]
+
+        def load_rows(src, name, tag):
+            raw = held([P, PACK, src.shape[1]], F32, name, tag)
+            nc.sync.dma_start(out=raw[:], in_=src.rearrange("(p t) c -> p t c", t=PACK))
+            return raw
+
+        def load_list(src, name):
+            offsets = keep.tile([P, S // 16], U16, name=name)
+            nc.sync.dma_start(offsets[:], src)
+            return offsets
+
+        def load_words(a):
+            words = held([P, T], I32, f"tab{a}", f"wide{a}")
+            nc.sync.dma_start(out=words[:], in_=tab_words[a].rearrange("p t i -> p (t i)").bitcast(I32))
+            return words
+
+        def load_plain(src, name):
+            tile = held([P, src.shape[1]], F32, name)
+            nc.sync.dma_start(out=tile[:], in_=src)
+            return tile
+
+        def load_per_row(src, name):
+            tile = held([P, H // PASS, PACK], F32, name)
+            nc.sync.dma_start(out=tile[:], in_=src.rearrange("(b p t) -> p b t", p=P, t=PACK))
+            return tile
+
+        def quantize(grouped, name):
+            width = grouped.shape[1] // PACK
+            codes = held([P, width], U32, name + "_codes")
+            scales = held([P, width], U8, name + "_scales")
+            nc.vector.quantize_mx(out=codes[:].bitcast(FP8X4), scales=scales[:], in_=grouped)
+            return codes, scales
+
+        def pairs_out(grouped):
+            return grouped.rearrange("p (c i t) -> p c t i", i=2, t=PACK)
+
+        def pairs_in(planes):
+            return planes.rearrange("p t (c i) -> p c t i", i=2)
+
+        tab_plane = held([P, T], U8, "tab_plane")
+        nc.vector.memset(tab_plane[:].bitcast(I32), 0)
+        w2_plane = held([P, 2, N], U8, "w2_plane")
+        nc.vector.memset(w2_plane[:].rearrange("p a n -> p (a n)").bitcast(I32), 0)
+        pages = [held([P, T2], F32, f"page{n}") for n in range(2)]
+        for page in pages:
+            nc.vector.memset(page[:], 0.0)
+
+        w1_raw = {}
+        w1_raw[0, 0] = load_rows(w1[0:PASS, 0:PASS], "w1_raw00", "slot0")
+        for q in range(4):
+            nc.sync.dma_start(
+                out=tab_plane[32 * q : 32 * q + 8, :].bitcast(I32),
+                in_=tab_scales[:, 4 * q : 4 * q + 4, :].bitcast(I32),
+            )
+        pick = load_list(offs, "pick")
+        tab = [load_words(0)]
+        w1_raw[1, 0] = load_rows(w1[PASS:K, 0:PASS], "w1_raw10", "slot1")
+        tab.append(load_words(1))
+        gains = load_per_row(gain, "gains")
+        put = load_list(offs2, "put")
+        put_weight = [load_plain(wgs[:, cols(half)], f"wgs{half}") for half in range(HALVES)]
+        for a in range(2):
+            w1_raw[a, 1] = load_rows(w1[a * PASS : (a + 1) * PASS, PASS:H], f"w1_raw{a}1", f"slot{2 + a}")
+        read = load_list(offs3, "read")
+        read_weight = load_plain(wgt, "wgt")
+        senses = load_per_row(sense, "senses")
+        w3_raw = [load_rows(w3[b * PASS : (b + 1) * PASS, :], f"w3_raw{b}", f"slot{4 + b}") for b in range(2)]
+        w2_codes = held([P, 2, 2 * N], U8, "w2_codes")
+        nc.sync.dma_start(out=w2_codes[:].bitcast(I32), in_=w2_words.rearrange("a p c -> p a c").bitcast(I32))
+        for q in range(4):
+            nc.sync.dma_start(
+                out=w2_plane[32 * q : 32 * q + 4, :, :].bitcast(I32),
+                in_=w2_scales[:, 4 * q : 4 * q + 4, :].rearrange("a r n -> r a n").bitcast(I32),
+            )
+
+        def quantize_w1(a, b):
+            grouped = ring.tile([P, PACK * PASS], BF16, name="grouped", align_bytes=64)
+            nc.scalar.copy(
+                out=grouped[:].rearrange("p (t m j) -> p m j t", t=PACK, j=PACK),
+                in_=w1_raw[a, b][:].rearrange("p j (m t) -> p m j t", t=PACK),
+            )
+            return quantize(grouped[:], f"w1_{a}{b}")
+
+        def gather_words(a, half):
+            picked = held([P, HALF], U32, f"picked{a}{half}")
+            nc.vector.tensor_copy(picked[:], tab[a][:].bitcast(U32).indirect(entries(pick, half)))
+            return picked
+
+        w1_q = {(0, 0): quantize_w1(0, 0)}
+        picked_plane = held([P, S], U8, "picked_plane")
+        nc.vector.tensor_copy(picked_plane[:], tab_plane[:].indirect(pick[:]))
+        picked = {(0, half): gather_words(0, half) for half in range(HALVES)}
+        w1_q[1, 0] = quantize_w1(1, 0)
+        for half in range(HALVES):
+            picked[1, half] = gather_words(1, half)
+
+        h = {(b, half): held([P, PACK, HALF], F32, f"h{b}{half}") for b in range(2) for half in range(HALVES)}
+
+        def features(b, t):
+            for half in range(HALVES):
+                acc = psum.tile([P, HALF], F32, name="acc")
+                for a in range(2):
+                    codes, scales = w1_q[a, b]
+                    nc.tensor.matmul_mx(
+                        out=acc[:],
+                        lhsT=codes[:, t * P : (t + 1) * P].bitcast(FP8X4),
+                        lhsT_scale=scales[:, t * P : (t + 1) * P],
+                        rhs=picked[a, half][:].bitcast(FP8X4),
+                        rhs_scale=picked_plane[4 * a : P, cols(half)],
+                        start=(a == 0),
+                        stop=(a == 1),
+                    )
+                plane = h[b, half][:, t, :]
+                nc.scalar.activation(out=plane, in_=acc[:], func=ACT.Tanh)
+                nc.scalar.activation(out=plane, in_=plane, func=ACT.Copy, scale=gains[:, b, t : t + 1])
+
+        for t in range(2):
+            features(0, t)
+        for a in range(2):
+            w1_q[a, 1] = quantize_w1(a, 1)
+        for t in range(2, PACK):
+            features(0, t)
+        for t in range(PACK):
+            features(1, t)
+
+        caps = [load_rows(cap[b * PASS : (b + 1) * PASS, :], f"cap{b}", f"wide{b}") for b in range(2)]
+
+        w3_q = []
+        for b in range(2):
+            grouped = ring.tile([P, PACK * N], BF16, name="grouped", align_bytes=64)
+            nc.scalar.copy(out=pairs_out(grouped[:]), in_=pairs_in(w3_raw[b][:]))
+            w3_q.append(quantize(grouped[:], f"w3_{b}"))
+        h_q = []
+        for b in range(2):
+            h_grouped = held([P, PACK * S], BF16, f"h_grouped{b}", f"slot{b}")
+            for half in range(HALVES):
+                nc.scalar.copy(
+                    out=pairs_out(h_grouped[:, half * PACK * HALF : (half + 1) * PACK * HALF]),
+                    in_=pairs_in(h[b, half][:]),
+                )
+            h_q.append(quantize(h_grouped[:], f"h_{b}"))
+        score = []
+        for half in range(HALVES):
+            need = held([P, N_TILES, HALF], F32, f"score{half}", f"slot{4 + half}")
+            for n in range(N_TILES):
+                acc = psum.tile([P, HALF], F32, name="acc")
+                for b in range(2):
+                    nc.tensor.matmul_mx(
+                        out=acc[:],
+                        lhsT=w3_q[b][0][:, n * P : (n + 1) * P].bitcast(FP8X4),
+                        lhsT_scale=w3_q[b][1][:, n * P : (n + 1) * P],
+                        rhs=h_q[b][0][:, cols(half)].bitcast(FP8X4),
+                        rhs_scale=h_q[b][1][:, cols(half)],
+                        start=(b == 0),
+                        stop=(b == 1),
+                    )
+                nc.scalar.copy(out=need[:, n, :], in_=acc[:])
+            score.append(need)
+
+        shrink = {
+            (b, half): held([P, PACK, HALF], F32, f"shrink{b}{half}", f"slot{2 * (1 - b) + half}")
+            for b in range(2)
+            for half in range(HALVES)
+        }
+
+        def scatter(row_tile, half):
+            b, t = divmod(row_tile, PACK)
+            page = pages[row_tile % 2]
+            nc.vector.tensor_tensor(
+                page[:].indirect(entries(put, half)), h[b, half][:, t, :], put_weight[half][:], ALU.mult
+            )
+
+        def gather(row_tile, half):
+            b, t = divmod(row_tile, PACK)
+            page = pages[row_tile % 2]
+            plane = shrink[b, half][:, t, :]
+            nc.vector.tensor_tensor(
+                plane, page[:].indirect(entries(read, half)), read_weight[:, cols(half)], ALU.mult
+            )
+            nc.scalar.activation(out=plane, in_=plane, func=ACT.Abs, scale=senses[:, b, t : t + 1])
+            nc.scalar.activation(out=plane, in_=plane, func=ACT.Abs_reciprocal_sqrt, bias=1.0)
+            nc.scalar.activation(out=plane, in_=plane, func=ACT.Square)
+
+        row_tiles = H // P
+        for step in range(row_tiles + 1):
+            for half in range(HALVES):
+                if step < row_tiles:
+                    scatter(step, half)
+                if step > 0:
+                    gather(step - 1, half)
+
+        z_q = {}
+        for b in range(2):
+            for half in range(HALVES):
+                grouped = ring.tile([P, PACK * HALF], BF16, name="grouped", align_bytes=64)
+                nc.vector.tensor_tensor(
+                    pairs_out(grouped[:]), pairs_in(shrink[b, half][:]), pairs_in(caps[b][:, :, cols(half)]), ALU.mult
+                )
+                z_q[b, half] = quantize(grouped[:], f"z_{b}{half}")
+        for half in range(HALVES):
+            for n in range(N_TILES):
+                acc = psum.tile([P, HALF], F32, name="acc")
+                for b in range(2):
+                    nc.tensor.matmul_mx(
+                        out=acc[:],
+                        lhsT=w2_codes[:, b, 2 * n * P : 2 * (n + 1) * P].bitcast(FP4X4),
+                        lhsT_scale=w2_plane[:, b, n * P : (n + 1) * P],
+                        rhs=z_q[b, half][0][:].bitcast(FP8X4),
+                        rhs_scale=z_q[b, half][1][:],
+                        start=(b == 0),
+                        stop=(b == 1),
+                    )
+                best = score[half][:, n, :]
+                nc.vector.tensor_tensor(best, acc[:], best, ALU.max)
+                nc.sync.dma_start(out=out[n * P : (n + 1) * P, cols(half)], in_=best)

@@ -23,6 +23,9 @@ HALF = 512
 HALVES = S // HALF
 LIST_COLS = HALF // 16
 N_TILES = N // P
+PAGES = 3
+HALF_PIECES = [(0, HALF), (HALF, S)]
+FIRST_PIECES = [(0, HALF // 2), (HALF // 2, HALF), (HALF, S)]
 
 
 def tile_list_locker_demand_scores_kernel(
@@ -85,12 +88,20 @@ def tile_list_locker_demand_scores_kernel(
         nc.vector.memset(tab_plane[:].bitcast(I32), 0)
         w2_plane = held([P, 2, N], U8, "w2_plane")
         nc.vector.memset(w2_plane[:].rearrange("p a n -> p (a n)").bitcast(I32), 0)
-        pages = [held([P, T2], F32, f"page{n}") for n in range(2)]
+        pages = [held([P, T2], F32, f"page{n}") for n in range(PAGES)]
         for page in pages:
             nc.vector.memset(page[:], 0.0)
 
-        w1_raw = {}
-        w1_raw[0, 0] = load_rows(w1[0:PASS, 0:PASS], "w1_raw00", "slot0")
+        w1_late = held([P, 2, PACK, PASS], F32, "w1_late", "twin1")
+        w1_raw = {(a, 0): held([P, PACK, PASS], F32, f"w1_first{a}", f"slot{a}")[:] for a in range(2)}
+        for a in range(2):
+            w1_raw[a, 1] = w1_late[:, a, :, :]
+
+        def load_w1(a, b):
+            rows = w1[a * PASS : (a + 1) * PASS, b * PASS : (b + 1) * PASS]
+            nc.sync.dma_start(out=w1_raw[a, b], in_=rows.rearrange("(p j) c -> p j c", j=PACK))
+
+        load_w1(0, 0)
         for q in range(4):
             nc.sync.dma_start(
                 out=tab_plane[32 * q : 32 * q + 8, :].bitcast(I32),
@@ -98,17 +109,19 @@ def tile_list_locker_demand_scores_kernel(
             )
         pick = load_list(offs, "pick")
         tab = [load_words(0)]
-        w1_raw[1, 0] = load_rows(w1[PASS:K, 0:PASS], "w1_raw10", "slot1")
+        load_w1(1, 0)
         tab.append(load_words(1))
         gains = load_per_row(gain, "gains")
         put = load_list(offs2, "put")
-        put_weight = [load_plain(wgs[:, cols(half)], f"wgs{half}") for half in range(HALVES)]
+        put_weight = held([P, S], F32, "wgs")
+        for half in range(HALVES):
+            nc.sync.dma_start(out=put_weight[:, cols(half)], in_=wgs[:, cols(half)])
         for a in range(2):
-            w1_raw[a, 1] = load_rows(w1[a * PASS : (a + 1) * PASS, PASS:H], f"w1_raw{a}1", f"slot{2 + a}")
+            load_w1(a, 1)
         read = load_list(offs3, "read")
         read_weight = load_plain(wgt, "wgt")
         senses = load_per_row(sense, "senses")
-        w3_raw = [load_rows(w3[b * PASS : (b + 1) * PASS, :], f"w3_raw{b}", f"slot{4 + b}") for b in range(2)]
+        w3_raw = [load_rows(w3[b * PASS : (b + 1) * PASS, :], f"w3_raw{b}", f"slot{2 + b}") for b in range(2)]
         w2_codes = held([P, 2, 2 * N], U8, "w2_codes")
         nc.sync.dma_start(out=w2_codes[:].bitcast(I32), in_=w2_words.rearrange("a p c -> p a c").bitcast(I32))
         for q in range(4):
@@ -121,7 +134,7 @@ def tile_list_locker_demand_scores_kernel(
             grouped = ring.tile([P, PACK * PASS], BF16, name="grouped", align_bytes=64)
             nc.scalar.copy(
                 out=grouped[:].rearrange("p (t m j) -> p m j t", t=PACK, j=PACK),
-                in_=w1_raw[a, b][:].rearrange("p j (m t) -> p m j t", t=PACK),
+                in_=w1_raw[a, b].rearrange("p j (m t) -> p m j t", t=PACK),
             )
             return quantize(grouped[:], f"w1_{a}{b}")
 
@@ -138,34 +151,36 @@ def tile_list_locker_demand_scores_kernel(
         for half in range(HALVES):
             picked[1, half] = gather_words(1, half)
 
-        h = {(b, half): held([P, PACK, HALF], F32, f"h{b}{half}") for b in range(2) for half in range(HALVES)}
+        h = [held([P, PACK, S], F32, f"h{b}") for b in range(2)]
 
-        def features(b, t):
-            for half in range(HALVES):
-                acc = psum.tile([P, HALF], F32, name="acc")
+        def features(b, t, pieces):
+            for lo, hi in pieces:
+                half, start = divmod(lo, HALF)
+                bank = psum.tile([P, HALF], F32, name="acc")
+                acc = bank[:, 0 : hi - lo]
                 for a in range(2):
                     codes, scales = w1_q[a, b]
                     nc.tensor.matmul_mx(
-                        out=acc[:],
+                        out=acc,
                         lhsT=codes[:, t * P : (t + 1) * P].bitcast(FP8X4),
                         lhsT_scale=scales[:, t * P : (t + 1) * P],
-                        rhs=picked[a, half][:].bitcast(FP8X4),
-                        rhs_scale=picked_plane[4 * a : P, cols(half)],
+                        rhs=picked[a, half][:, start : start + hi - lo].bitcast(FP8X4),
+                        rhs_scale=picked_plane[4 * a : P, lo:hi],
                         start=(a == 0),
                         stop=(a == 1),
                     )
-                plane = h[b, half][:, t, :]
-                nc.scalar.activation(out=plane, in_=acc[:], func=ACT.Tanh)
+                plane = h[b][:, t, lo:hi]
+                nc.scalar.activation(out=plane, in_=acc, func=ACT.Tanh)
                 nc.scalar.activation(out=plane, in_=plane, func=ACT.Copy, scale=gains[:, b, t : t + 1])
 
-        for t in range(2):
-            features(0, t)
+        features(0, 0, FIRST_PIECES)
+        features(0, 1, HALF_PIECES)
         for a in range(2):
             w1_q[a, 1] = quantize_w1(a, 1)
         for t in range(2, PACK):
-            features(0, t)
+            features(0, t, HALF_PIECES)
         for t in range(PACK):
-            features(1, t)
+            features(1, t, HALF_PIECES)
 
         caps = [load_rows(cap[b * PASS : (b + 1) * PASS, :], f"cap{b}", f"wide{b}") for b in range(2)]
 
@@ -175,72 +190,68 @@ def tile_list_locker_demand_scores_kernel(
             nc.scalar.copy(out=pairs_out(grouped[:]), in_=pairs_in(w3_raw[b][:]))
             w3_q.append(quantize(grouped[:], f"w3_{b}"))
         h_q = []
+        h_grouped = held([P, 2, PACK * S], BF16, "h_grouped", "twin0")
         for b in range(2):
-            h_grouped = held([P, PACK * S], BF16, f"h_grouped{b}", f"slot{b}")
-            for half in range(HALVES):
-                nc.scalar.copy(
-                    out=pairs_out(h_grouped[:, half * PACK * HALF : (half + 1) * PACK * HALF]),
-                    in_=pairs_in(h[b, half][:]),
-                )
-            h_q.append(quantize(h_grouped[:], f"h_{b}"))
-        score = []
-        for half in range(HALVES):
-            need = held([P, N_TILES, HALF], F32, f"score{half}", f"slot{4 + half}")
-            for n in range(N_TILES):
-                acc = psum.tile([P, HALF], F32, name="acc")
-                for b in range(2):
-                    nc.tensor.matmul_mx(
-                        out=acc[:],
-                        lhsT=w3_q[b][0][:, n * P : (n + 1) * P].bitcast(FP8X4),
-                        lhsT_scale=w3_q[b][1][:, n * P : (n + 1) * P],
-                        rhs=h_q[b][0][:, cols(half)].bitcast(FP8X4),
-                        rhs_scale=h_q[b][1][:, cols(half)],
-                        start=(b == 0),
-                        stop=(b == 1),
-                    )
-                nc.scalar.copy(out=need[:, n, :], in_=acc[:])
-            score.append(need)
+            nc.scalar.copy(out=pairs_out(h_grouped[:, b, :]), in_=pairs_in(h[b][:]))
+            h_q.append(quantize(h_grouped[:, b, :], f"h_{b}"))
+        shrink = [held([P, PACK, S], F32, f"shrink{b}", f"twin{1 - b}") for b in range(2)]
 
-        shrink = {
-            (b, half): held([P, PACK, HALF], F32, f"shrink{b}{half}", f"slot{2 * (1 - b) + half}")
-            for b in range(2)
-            for half in range(HALVES)
-        }
-
-        def scatter(row_tile, half):
+        def scatter(row_tile, offsets, columns):
             b, t = divmod(row_tile, PACK)
-            page = pages[row_tile % 2]
-            nc.vector.tensor_tensor(
-                page[:].indirect(entries(put, half)), h[b, half][:, t, :], put_weight[half][:], ALU.mult
-            )
+            page = pages[row_tile % PAGES]
+            nc.vector.tensor_tensor(page[:].indirect(offsets), h[b][:, t, columns], put_weight[:, columns], ALU.mult)
 
-        def gather(row_tile, half):
+        def gather(row_tile):
             b, t = divmod(row_tile, PACK)
-            page = pages[row_tile % 2]
-            plane = shrink[b, half][:, t, :]
-            nc.vector.tensor_tensor(
-                plane, page[:].indirect(entries(read, half)), read_weight[:, cols(half)], ALU.mult
-            )
+            page = pages[row_tile % PAGES]
+            plane = shrink[b][:, t, :]
+            nc.vector.tensor_tensor(plane, page[:].indirect(read[:]), read_weight[:], ALU.mult)
             nc.scalar.activation(out=plane, in_=plane, func=ACT.Abs, scale=senses[:, b, t : t + 1])
-            nc.scalar.activation(out=plane, in_=plane, func=ACT.Abs_reciprocal_sqrt, bias=1.0)
-            nc.scalar.activation(out=plane, in_=plane, func=ACT.Square)
+            nc.scalar.activation(out=plane, in_=plane, func=ACT.Abs_reciprocal_sqrt, bias=2.25, scale=2.25)
+            nc.scalar.activation(out=plane, in_=plane, func=ACT.Square, scale=1.5)
+
+        score = []
+
+        def need_scores():
+            for half in range(HALVES):
+                need = held([P, N_TILES, HALF], F32, f"score{half}", f"slot{2 + half}")
+                for n in range(N_TILES):
+                    acc = psum.tile([P, HALF], F32, name="acc")
+                    for b in range(2):
+                        nc.tensor.matmul_mx(
+                            out=acc[:],
+                            lhsT=w3_q[b][0][:, n * P : (n + 1) * P].bitcast(FP8X4),
+                            lhsT_scale=w3_q[b][1][:, n * P : (n + 1) * P],
+                            rhs=h_q[b][0][:, cols(half)].bitcast(FP8X4),
+                            rhs_scale=h_q[b][1][:, cols(half)],
+                            start=(b == 0),
+                            stop=(b == 1),
+                        )
+                    nc.scalar.copy(out=need[:, n, :], in_=acc[:])
+                score.append(need)
 
         row_tiles = H // P
-        for step in range(row_tiles + 1):
-            for half in range(HALVES):
-                if step < row_tiles:
-                    scatter(step, half)
-                if step > 0:
-                    gather(step - 1, half)
+        for lo, hi in FIRST_PIECES:
+            scatter(0, put[:, lo // 16 : hi // 16], slice(lo, hi))
+        for row_tile in range(1, row_tiles):
+            scatter(row_tile, put[:], slice(0, S))
+            gather(row_tile - 1)
+            if row_tile == PACK:
+                need_scores()
+        gather(row_tiles - 1)
 
         z_q = {}
         for b in range(2):
+            z_grouped = held([P, HALVES * PACK * HALF], BF16, f"z_grouped{b}", f"page{(row_tiles - 1 - b) % PAGES}")
             for half in range(HALVES):
-                grouped = ring.tile([P, PACK * HALF], BF16, name="grouped", align_bytes=64)
                 nc.vector.tensor_tensor(
-                    pairs_out(grouped[:]), pairs_in(shrink[b, half][:]), pairs_in(caps[b][:, :, cols(half)]), ALU.mult
+                    pairs_out(z_grouped[:, half * PACK * HALF : (half + 1) * PACK * HALF]),
+                    pairs_in(shrink[b][:, :, cols(half)]),
+                    pairs_in(caps[b][:, :, cols(half)]),
+                    ALU.mult,
                 )
-                z_q[b, half] = quantize(grouped[:], f"z_{b}{half}")
+            for half in range(HALVES):
+                z_q[b, half] = quantize(z_grouped[:, half * PACK * HALF : (half + 1) * PACK * HALF], f"z_{b}{half}")
         for half in range(HALVES):
             for n in range(N_TILES):
                 acc = psum.tile([P, HALF], F32, name="acc")

from contextlib import ExitStack

import concourse.mybir as mybir

K, H, N, T, S, T2 = 1024, 1024, 512, 4096, 1024, 2048
FLOPS = 2 * K * H * S + 2 * 2 * H * N * S

F32 = mybir.dt.float32
BF16 = mybir.dt.bfloat16
I32 = mybir.dt.int32
U32 = mybir.dt.uint32
U16 = mybir.dt.uint16
U8 = mybir.dt.uint8
FP8X4 = mybir.dt.float8_e4m3fn_x4
FP4X4 = mybir.dt.float4_e2m1fn_x4
ACT = mybir.ActivationFunctionType
ALU = mybir.AluOpType

P = 128
PACK = 4
PASS = P * PACK
HALF = 512
HALVES = S // HALF
LIST_COLS = HALF // 16
N_TILES = N // P
PAGES = 3
HALF_PIECES = [(0, HALF), (HALF, S)]
FIRST_PIECES = [(0, HALF // 2), (HALF // 2, HALF), (HALF, S)]


def tile_list_locker_demand_scores_kernel(
    tc, tab_words, tab_scales, offs, offs2, offs3, w1, gain, wgs, wgt, sense, cap, w2_words, w2_scales, w3, out
):
    nc = tc.nc
    with ExitStack() as ctx:
        keep = ctx.enter_context(tc.tile_pool(name="keep", bufs=1))
        ring = ctx.enter_context(tc.tile_pool(name="ring", bufs=2))
        psum = ctx.enter_context(tc.psum_pool(name="psum", bufs=8))

        def held(shape, dtype, name, tag=None):
            return keep.tile(shape, dtype, name=name, tag=tag or name, align_bytes=64)

        def cols(half):
            return slice(half * HALF, (half + 1) * HALF)

        def entries(offsets, half):
            return offsets[:, half * LIST_COLS : (half + 1) * LIST_COLS]

        def load_rows(src, name, tag):
            raw = held([P, PACK, src.shape[1]], F32, name, tag)
            nc.sync.dma_start(out=raw[:], in_=src.rearrange("(p t) c -> p t c", t=PACK))
            return raw

        def load_list(src, name):
            offsets = keep.tile([P, S // 16], U16, name=name)
            nc.sync.dma_start(offsets[:], src)
            return offsets

        def load_words(a):
            words = held([P, T], I32, f"tab{a}", f"wide{a}")
            nc.sync.dma_start(out=words[:], in_=tab_words[a].rearrange("p t i -> p (t i)").bitcast(I32))
            return words

        def load_plain(src, name):
            tile = held([P, src.shape[1]], F32, name)
            nc.sync.dma_start(out=tile[:], in_=src)
            return tile

        def load_per_row(src, name):
            tile = held([P, H // PASS, PACK], F32, name)
            nc.sync.dma_start(out=tile[:], in_=src.rearrange("(b p t) -> p b t", p=P, t=PACK))
            return tile

        def quantize(grouped, name):
            width = grouped.shape[1] // PACK
            codes = held([P, width], U32, name + "_codes")
            scales = held([P, width], U8, name + "_scales")
            nc.vector.quantize_mx(out=codes[:].bitcast(FP8X4), scales=scales[:], in_=grouped)
            return codes, scales

        def pairs_out(grouped):
            return grouped.rearrange("p (c i t) -> p c t i", i=2, t=PACK)

        def pairs_in(planes):
            return planes.rearrange("p t (c i) -> p c t i", i=2)

        tab_plane = held([P, T], U8, "tab_plane")
        nc.vector.memset(tab_plane[:].bitcast(I32), 0)
        w2_plane = held([P, 2, N], U8, "w2_plane")
        nc.vector.memset(w2_plane[:].rearrange("p a n -> p (a n)").bitcast(I32), 0)
        pages = [held([P, T2], F32, f"page{n}") for n in range(PAGES)]
        for page in pages:
            nc.vector.memset(page[:], 0.0)

        w1_late = held([P, 2, PACK, PASS], F32, "w1_late", "twin1")
        w1_raw = {(a, 0): held([P, PACK, PASS], F32, f"w1_first{a}", f"slot{a}")[:] for a in range(2)}
        for a in range(2):
            w1_raw[a, 1] = w1_late[:, a, :, :]

        def load_w1(a, b):
            rows = w1[a * PASS : (a + 1) * PASS, b * PASS : (b + 1) * PASS]
            nc.sync.dma_start(out=w1_raw[a, b], in_=rows.rearrange("(p j) c -> p j c", j=PACK))

        load_w1(0, 0)
        for q in range(4):
            nc.sync.dma_start(
                out=tab_plane[32 * q : 32 * q + 8, :].bitcast(I32),
                in_=tab_scales[:, 4 * q : 4 * q + 4, :].bitcast(I32),
            )
        pick = load_list(offs, "pick")
        tab = [load_words(0)]
        load_w1(1, 0)
        tab.append(load_words(1))
        gains = load_per_row(gain, "gains")
        put = load_list(offs2, "put")
        put_weight = held([P, S], F32, "wgs")
        for half in range(HALVES):
            nc.sync.dma_start(out=put_weight[:, cols(half)], in_=wgs[:, cols(half)])
        for a in range(2):
            load_w1(a, 1)
        read = load_list(offs3, "read")
        read_weight = load_plain(wgt, "wgt")
        senses = load_per_row(sense, "senses")
        w3_raw = [load_rows(w3[b * PASS : (b + 1) * PASS, :], f"w3_raw{b}", f"slot{2 + b}") for b in range(2)]
        w2_codes = held([P, 2, 2 * N], U8, "w2_codes")
        nc.sync.dma_start(out=w2_codes[:].bitcast(I32), in_=w2_words.rearrange("a p c -> p a c").bitcast(I32))
        for q in range(4):
            nc.sync.dma_start(
                out=w2_plane[32 * q : 32 * q + 4, :, :].bitcast(I32),
                in_=w2_scales[:, 4 * q : 4 * q + 4, :].rearrange("a r n -> r a n").bitcast(I32),
            )

        def quantize_w1(a, b):
            grouped = ring.tile([P, PACK * PASS], BF16, name="grouped", align_bytes=64)
            nc.scalar.copy(
                out=grouped[:].rearrange("p (t m j) -> p m j t", t=PACK, j=PACK),
                in_=w1_raw[a, b].rearrange("p j (m t) -> p m j t", t=PACK),
            )
            return quantize(grouped[:], f"w1_{a}{b}")

        def gather_words(a, half):
            picked = held([P, HALF], U32, f"picked{a}{half}")
            nc.vector.tensor_copy(picked[:], tab[a][:].bitcast(U32).indirect(entries(pick, half)))
            return picked

        w1_q = {(0, 0): quantize_w1(0, 0)}
        picked_plane = held([P, S], U8, "picked_plane")
        nc.vector.tensor_copy(picked_plane[:], tab_plane[:].indirect(pick[:]))
        picked = {(0, half): gather_words(0, half) for half in range(HALVES)}
        w1_q[1, 0] = quantize_w1(1, 0)
        for half in range(HALVES):
            picked[1, half] = gather_words(1, half)

        h = [held([P, PACK, S], F32, f"h{b}") for b in range(2)]

        def features(b, t, pieces):
            for lo, hi in pieces:
                half, start = divmod(lo, HALF)
                bank = psum.tile([P, HALF], F32, name="acc")
                acc = bank[:, 0 : hi - lo]
                for a in range(2):
                    codes, scales = w1_q[a, b]
                    nc.tensor.matmul_mx(
                        out=acc,
                        lhsT=codes[:, t * P : (t + 1) * P].bitcast(FP8X4),
                        lhsT_scale=scales[:, t * P : (t + 1) * P],
                        rhs=picked[a, half][:, start : start + hi - lo].bitcast(FP8X4),
                        rhs_scale=picked_plane[4 * a : P, lo:hi],
                        start=(a == 0),
                        stop=(a == 1),
                    )
                plane = h[b][:, t, lo:hi]
                nc.scalar.activation(out=plane, in_=acc, func=ACT.Tanh)
                nc.scalar.activation(out=plane, in_=plane, func=ACT.Copy, scale=gains[:, b, t : t + 1])

        features(0, 0, FIRST_PIECES)
        features(0, 1, HALF_PIECES)
        for a in range(2):
            w1_q[a, 1] = quantize_w1(a, 1)
        for t in range(2, PACK):
            features(0, t, HALF_PIECES)
        for t in range(PACK):
            features(1, t, HALF_PIECES)

        caps = [load_rows(cap[b * PASS : (b + 1) * PASS, :], f"cap{b}", f"wide{b}") for b in range(2)]

        w3_q = []
        for b in range(2):
            grouped = ring.tile([P, PACK * N], BF16, name="grouped", align_bytes=64)
            nc.scalar.copy(out=pairs_out(grouped[:]), in_=pairs_in(w3_raw[b][:]))
            w3_q.append(quantize(grouped[:], f"w3_{b}"))
        h_q = []
        h_grouped = held([P, 2, PACK * S], BF16, "h_grouped", "twin0")
        for b in range(2):
            nc.scalar.copy(out=pairs_out(h_grouped[:, b, :]), in_=pairs_in(h[b][:]))
            h_q.append(quantize(h_grouped[:, b, :], f"h_{b}"))
        shrink = [held([P, PACK, S], F32, f"shrink{b}", f"twin{1 - b}") for b in range(2)]

        def scatter(row_tile, offsets, columns):
            b, t = divmod(row_tile, PACK)
            page = pages[row_tile % PAGES]
            nc.vector.tensor_tensor(page[:].indirect(offsets), h[b][:, t, columns], put_weight[:, columns], ALU.mult)

        def gather(row_tile):
            b, t = divmod(row_tile, PACK)
            page = pages[row_tile % PAGES]
            plane = shrink[b][:, t, :]
            nc.vector.tensor_tensor(plane, page[:].indirect(read[:]), read_weight[:], ALU.mult)
            nc.scalar.activation(out=plane, in_=plane, func=ACT.Abs, scale=senses[:, b, t : t + 1])
            nc.scalar.activation(out=plane, in_=plane, func=ACT.Abs_reciprocal_sqrt, bias=2.25, scale=2.25)
            nc.scalar.activation(out=plane, in_=plane, func=ACT.Square, scale=1.5)

        score = []

        def need_scores():
            for half in range(HALVES):
                need = held([P, N_TILES, HALF], F32, f"score{half}", f"slot{2 + half}")
                for n in range(N_TILES):
                    acc = psum.tile([P, HALF], F32, name="acc")
                    for b in range(2):
                        nc.tensor.matmul_mx(
                            out=acc[:],
                            lhsT=w3_q[b][0][:, n * P : (n + 1) * P].bitcast(FP8X4),
                            lhsT_scale=w3_q[b][1][:, n * P : (n + 1) * P],
                            rhs=h_q[b][0][:, cols(half)].bitcast(FP8X4),
                            rhs_scale=h_q[b][1][:, cols(half)],
                            start=(b == 0),
                            stop=(b == 1),
                        )
                    nc.scalar.copy(out=need[:, n, :], in_=acc[:])
                score.append(need)

        row_tiles = H // P
        for lo, hi in FIRST_PIECES:
            scatter(0, put[:, lo // 16 : hi // 16], slice(lo, hi))
        for row_tile in range(1, row_tiles):
            scatter(row_tile, put[:], slice(0, S))
            gather(row_tile - 1)
            if row_tile == PACK:
                need_scores()
        gather(row_tiles - 1)

        z_q = {}
        for b in range(2):
            z_grouped = held([P, HALVES * PACK * HALF], BF16, f"z_grouped{b}", f"page{(row_tiles - 1 - b) % PAGES}")
            for half in range(HALVES):
                nc.vector.tensor_tensor(
                    pairs_out(z_grouped[:, half * PACK * HALF : (half + 1) * PACK * HALF]),
                    pairs_in(shrink[b][:, :, cols(half)]),
                    pairs_in(caps[b][:, :, cols(half)]),
                    ALU.mult,
                )
            for half in range(HALVES):
                z_q[b, half] = quantize(z_grouped[:, half * PACK * HALF : (half + 1) * PACK * HALF], f"z_{b}{half}")
        for half in range(HALVES):
            for n in range(N_TILES):
                acc = psum.tile([P, HALF], F32, name="acc")
                for b in range(2):
                    nc.tensor.matmul_mx(
                        out=acc[:],
                        lhsT=w2_codes[:, b, 2 * n * P : 2 * (n + 1) * P].bitcast(FP4X4),
                        lhsT_scale=w2_plane[:, b, n * P : (n + 1) * P],
                        rhs=z_q[b, half][0][:].bitcast(FP8X4),
                        rhs_scale=z_q[b, half][1][:],
                        start=(b == 0),
                        stop=(b == 1),
                    )
                best = score[half][:, n, :]
                nc.vector.tensor_tensor(best, acc[:], best, ALU.max)
                nc.sync.dma_start(out=out[n * P : (n + 1) * P, cols(half)], in_=best)
